import numpy as np
import ml_dtypes


def mxq(x, axis, fmt="e4m3"):
    dtype, down = {"e4m3": (ml_dtypes.float8_e4m3fn, 7), "e5m2": (ml_dtypes.float8_e5m2, 14)}[fmt]
    v = np.moveaxis(np.asarray(x, np.float32).astype(ml_dtypes.bfloat16).astype(np.float64), axis, -1)
    blocks = v.reshape(v.shape[:-1] + (-1, 32))
    amax = np.abs(blocks).max(-1, keepdims=True)
    byte = np.maximum(np.where(amax > 0, np.frexp(amax)[1] - 1 + 127, 0) - down, 1)
    scale = np.exp2(byte - 127.0)
    codes = (blocks / scale).astype(np.float32).astype(dtype).astype(np.float64)
    return np.moveaxis((codes * scale).reshape(v.shape), -1, axis)


WIDE = False


def mx_kscale(k):
    if not WIDE:
        return np.ones(k)
    levels = np.array([10, -10, 5, -5, 0])
    if k % 512:
        return np.exp2(np.random.permutation(np.resize(levels, k // 32))).repeat(32)
    a = np.empty((k // 512, 16))
    for p in range(k // 512):
        a[p, :8] = np.random.permutation(np.resize(levels, 8))
        for g in range(8):
            far = levels[np.abs(levels - a[p, g]) >= 10]
            a[p, g + 8] = far[np.random.randint(len(far))]
    return np.exp2(a.ravel()).repeat(32)


def f64(x):
    return np.asarray(x).astype(np.float64)


def striped(idx):
    return np.tile(idx.reshape(-1, 16).T, (8, 1)).astype(np.uint16)


def unstriped(offs):
    return offs[:16].T.reshape(-1).astype(np.int64)


def striped8(idx):
    return np.concatenate([x.reshape(-1, 16).T for x in idx]).astype(np.uint16)


def runs(offs, k):
    lists = np.stack([offs[16 * r : 16 * r + 16].T.reshape(-1) for r in range(8)]).astype(np.int64)
    return lists[np.arange(k) % 512 // 64]


def pack_weight(w):
    k, n = w.shape
    w = f64(np.asarray(w, np.float32).astype(ml_dtypes.bfloat16)).reshape(k // 32, 32, n)
    amax = np.abs(w).max(1)
    byte = np.clip(np.where(amax > 0, np.frexp(amax)[1] - 1 + 127 - 7, 1), 1, 254)
    scaled = (w * np.exp2(127.0 - byte)[:, None, :]).reshape(k, n).astype(np.float32)
    words = np.ascontiguousarray(scaled.reshape(k // 512, 128, 4, n).transpose(0, 1, 3, 2)).astype(ml_dtypes.float8_e4m3fn).view(np.uint8)
    return words, np.ascontiguousarray(byte.astype(np.uint8).reshape(k // 512, 16, n))


def unpack_weight(words, scales):
    g, p, n, _ = words.shape
    vals = np.ascontiguousarray(words).view(ml_dtypes.float8_e4m3fn).astype(np.float64) * np.repeat(np.exp2(scales.astype(np.float64) - 127.0), 8, axis=1)[..., None]
    return vals.transpose(0, 1, 3, 2).reshape(g * 512, n)


def relu(v):
    return np.maximum(v, 0.0)


K, T, S, V, N, H = 512, 2048, 512, 256, 512, 512


def setup_inputs():
    n = np.random.standard_normal
    s = mx_kscale(K)[:, None]
    u = mx_kscale(H)
    packed_xT = pack_weight(n((K, T)) * s)
    return {
        "x_words": packed_xT[0],
        "x_scales": packed_xT[1],
        "w1": (n((K, H)) / np.sqrt(K) / s * u).astype(np.float32),
        "w2": (n((H, H)) / np.sqrt(H) / u[:, None] * u).astype(np.float32),
        "w3": (n((H, N)) / np.sqrt(H) / u[:, None]).astype(np.float32),
        "res": n((N, S)).astype(np.float32),
        "offs": striped(np.random.permutation(T)[:S]),
        "order": striped8(np.stack([np.random.permutation(S) for _ in range(8)])),
        "at": striped8(np.stack([np.random.permutation(S)[:V] for _ in range(8)])),
    }


def reference(x_words, x_scales, w1, w2, w3, res, offs, order, at):
    xq = unpack_weight(x_words, x_scales)[:, unstriped(offs)]
    y = mxq(f64(w1), 0, "e4m3").T @ xq
    o = y[np.arange(H)[:, None], runs(order, H)]
    z = o.reshape(H, V, 2).max(axis=2)
    h = relu(mxq(f64(w2), 0, "e4m3").T @ mxq(z, 0, "e4m3"))
    z2 = y.copy()
    z2[np.arange(H)[:, None], runs(at, H)] = h
    return f64(res) + (mxq(f64(w3), 0, "e4m3").T @ mxq(z2, 0, "e4m3"))

@@ -1,0 +1,188 @@
+from contextlib import ExitStack
+
+import concourse.mybir as mybir
+
+K, T, S, V, N, H = 512, 2048, 512, 256, 512, 512
+FLOPS = 2 * K * H * S + 2 * H * H * V + 2 * H * N * S
+
+F32 = mybir.dt.float32
+BF16 = mybir.dt.bfloat16
+I32 = mybir.dt.int32
+U32 = mybir.dt.uint32
+U16 = mybir.dt.uint16
+U8 = mybir.dt.uint8
+FP8X4 = mybir.dt.float8_e4m3fn_x4
+MAX = mybir.AluOpType.max
+ADD = mybir.AluOpType.add
+RELU = mybir.ActivationFunctionType.Relu
+
+P = 128
+PACK = 4
+
+
+def tile_picked_poolback_none_p_kernel(tc, x_words, x_scales, w1, w2, w3, res, offs, order, at, out):
+    nc = tc.nc
+    with ExitStack() as ctx:
+        lists = ctx.enter_context(tc.tile_pool(name="lists", bufs=1))
+        keep = ctx.enter_context(tc.tile_pool(name="keep", bufs=1))
+        psum = ctx.enter_context(tc.psum_pool(name="psum", bufs=1))
+
+        def sb(name, shape, dtype):
+            return keep.tile(shape, dtype, name=name, align_bytes=64)
+
+        xs = sb("xs", [P, T], U8)
+        nc.vector.memset(xs[:].bitcast(I32), 0)
+        xw = sb("xw", [P, T], I32)
+        nc.sync.dma_start(out=xw[:], in_=x_words[0].rearrange("p n t -> p (n t)").bitcast(I32))
+        for q in range(4):
+            nc.sync.dma_start(out=xs[32 * q : 32 * q + 4, :].bitcast(I32), in_=x_scales[0, 4 * q : 4 * q + 4, :].bitcast(I32))
+        offs_t = lists.tile([P, S // 16], U16, name="offs_t")
+        nc.sync.dma_start(offs_t[:], offs)
+
+        def load_half(name, w, a):
+            raw = sb("%s_raw%d" % (name, a), [P, PACK, H // 2], F32)
+            nc.sync.dma_start(out=raw[:], in_=w.rearrange("(p j) c -> p j c", j=PACK)[:, :, a * 256 : (a + 1) * 256])
+            return raw
+
+        w1_raw = [load_half("w1", w1, a) for a in range(2)]
+        order_t = lists.tile([P, S // 16], U16, name="order_t")
+        nc.sync.dma_start(order_t[:], order)
+        w2_raw = [load_half("w2", w2, 0)]
+        at_t = lists.tile([P, V // 16], U16, name="at_t")
+        nc.sync.dma_start(at_t[:], at)
+        res_rows = res.rearrange("(t p) s -> p t s", p=P)
+        res_t = sb("res_t", [P, PACK, S], F32)
+        nc.sync.dma_start(out=res_t[:, 0, :], in_=res_rows[:, 0, :])
+        w2_raw.append(load_half("w2", w2, 1))
+        w3_raw = sb("w3_raw", [P, PACK, N], F32)
+        nc.sync.dma_start(out=w3_raw[:], in_=w3.rearrange("(p j) c -> p j c", j=PACK))
+        nc.sync.dma_start(out=res_t[:, 1:, :], in_=res_rows[:, 1:, :])
+
+        xg_s = sb("xg_s", [P, S], U8)
+        xg_w = sb("xg_w", [P, S], U32)
+        nc.vector.tensor_copy(xg_w[:], xw[:].bitcast(U32).indirect(offs_t[:]))
+        nc.vector.tensor_copy(xg_s[:], xs[:].indirect(offs_t[:]))
+
+        def deal(copy, dst, raw, a, t0, t1):
+            copy(
+                out=dst.rearrange("p i m j -> p m j i")[:, 64 * a : 64 * a + 64],
+                in_=raw[:].rearrange("p j (m t) -> p m j t", t=PACK)[:, :, :, t0:t1],
+            )
+
+        def quantize(codes, scales, src):
+            nc.vector.quantize_mx(out=codes.bitcast(FP8X4), scales=scales, in_=src)
+
+        def bank(i, shape):
+            return psum.tile(shape, F32, name="bank%d" % i)
+
+        def mm(acc, wc, ws, t, rc, rs):
+            nc.tensor.matmul_mx(out=acc, lhsT=wc[:, t * P : (t + 1) * P].bitcast(FP8X4), lhsT_scale=ws[:, t * P : (t + 1) * P],
+                                rhs=rc.bitcast(FP8X4), rhs_scale=rs, start=True, stop=True)
+
+        w1_b = [sb("dealt", [P, 2, P, PACK], BF16), sb("w1_b1", [P, 2, P, PACK], BF16)]
+        deal(nc.scalar.copy, w1_b[0][:], w1_raw[0], 0, 0, 2)
+        deal(nc.scalar.copy, w1_b[1][:], w1_raw[0], 0, 2, 4)
+        deal(nc.vector.tensor_copy, w1_b[0][:], w1_raw[1], 1, 0, 2)
+        deal(nc.scalar.copy, w1_b[1][:], w1_raw[1], 1, 2, 4)
+        w1_c = sb("w1_c", [P, H], U32)
+        w1_s = sb("w1_s", [P, H], U8)
+        for t0, t1 in [(0, 1), (1, 2), (2, 4)]:
+            quantize(w1_c[:, t0 * P : t1 * P], w1_s[:, t0 * P : t1 * P],
+                     w1_b[t0 // 2][:, t0 % 2 : t0 % 2 + t1 - t0].rearrange("p i m j -> p (i m j)"))
+        SH = S // 2
+        y = [sb("y%d" % t, [P, S], F32) for t in range(PACK)]
+        for b in range(2):
+            cols = slice(b * SH, (b + 1) * SH)
+            acc = bank(4 * b, [P, SH])
+            mm(acc[:], w1_c, w1_s, 0, xg_w[:, cols], xg_s[:, cols])
+            nc.scalar.copy(out=y[0][:, cols], in_=acc[:])
+        for t in range(1, PACK):
+            acc = bank(t, [P, S])
+            mm(acc[:], w1_c, w1_s, t, xg_w[:], xg_s[:])
+            nc.scalar.copy(out=y[t][:], in_=acc[:])
+
+        w2_b = sb("dealt", [P, PACK, P, PACK], BF16)
+        deal(nc.vector.tensor_copy, w2_b[:], w2_raw[0], 0, 0, 4)
+        deal(nc.scalar.copy, w2_b[:], w2_raw[1], 1, 0, 4)
+        w2_c = sb("w2_c", [P, H], U32)
+        w2_s = sb("w2_s", [P, H], U8)
+
+        w3_b = sb("w3_b", [P, N, PACK], BF16)
+        for a in range(4):
+            nc.scalar.copy(
+                out=w3_b[:, a * P : (a + 1) * P, :].rearrange("p (c i) j -> p c j i", i=4),
+                in_=w3_raw[:, :, a * P : (a + 1) * P].rearrange("p j (c i) -> p c j i", i=4),
+            )
+
+        VH = V // 2
+        quantize(w2_c[:], w2_s[:], w2_b[:].rearrange("p t m j -> p (t m j)"))
+        h = sb("h", [P, PACK, V], F32)
+        g = sb("g", [P, PACK, 2 * VH], BF16)
+        z = [sb("z%d" % a, [P, VH, PACK], BF16) for a in range(2)]
+
+        def gather(a, t):
+            nc.vector.tensor_copy(g[:, t, :], y[t][:].indirect(order_t[:, 16 * a : 16 * a + 16]))
+
+        def pool_pairs(a):
+            pairs = g[:].rearrange("p t (c i e) -> p c t i e", i=4, e=2)
+            nc.vector.tensor_tensor(z[a][:].rearrange("p (c i) t -> p c t i", i=4), pairs[:, :, :, :, 0], pairs[:, :, :, :, 1], MAX)
+
+        def second(a):
+            z_c = sb("z_c%d" % a, [P, VH], U32)
+            z_s = sb("z_s%d" % a, [P, VH], U8)
+            quantize(z_c[:], z_s[:], z[a][:].rearrange("p v t -> p (v t)"))
+            for i, (t0, t1) in enumerate([(0, PACK)] if a == 0 else [(0, 1), (1, PACK)]):
+                acc = bank(5 + a + i, [P, t1 - t0, VH])
+                for t in range(t0, t1):
+                    mm(acc[:, t - t0, :], w2_c, w2_s, t, z_c[:], z_s[:])
+                nc.scalar.activation(h[:, t0:t1, a * VH : (a + 1) * VH], acc[:], RELU)
+
+        for t in range(PACK):
+            gather(0, t)
+        pool_pairs(0)
+        gather(1, 0)
+        second(0)
+        for t in range(1, PACK):
+            gather(1, t)
+        pool_pairs(1)
+        second(1)
+
+        w3_c = sb("w3_c", [P, N], U32)
+        w3_s = sb("w3_s", [P, N], U8)
+        quantize(w3_c[:], w3_s[:], w3_b[:].rearrange("p n j -> p (n j)"))
+
+        z2 = [sb("z2_%d" % b, [P, SH, PACK], BF16) for b in range(2)]
+
+        def scatter(t, v0, v1):
+            nc.vector.tensor_copy(y[t][:].indirect(at_t[:, v0 // 16 : v1 // 16]), h[:, t, v0:v1])
+
+        def weave(copy, b, t):
+            copy(out=z2[b][:, :, t], in_=y[t][:, b * SH : (b + 1) * SH])
+
+        scatter(0, 0, VH)
+        scatter(0, VH, V)
+        for t in range(PACK):
+            if t > 0:
+                scatter(t, 0, V)
+            if t == 2:
+                nc.scalar.copy(out=z2[0][:, :, 2:4], in_=y[2][:, :SH].unsqueeze(2).to_broadcast([P, SH, 2]))
+            elif t == 3:
+                weave(nc.vector.tensor_copy, 0, t)
+            else:
+                weave(nc.scalar.copy, 0, t)
+            weave(nc.scalar.copy, 1, t)
+
+        out_rows = out.rearrange("(t p) s -> p t s", p=P)
+        z2_c = [sb("z2_c%d" % b, [P, SH], U32) for b in range(2)]
+        z2_s = [sb("z2_s%d" % b, [P, SH], U8) for b in range(2)]
+        for b in range(2):
+            quantize(z2_c[b][:], z2_s[b][:], z2[b][:].rearrange("p s t -> p (s t)"))
+        pieces = [(0, 0, 1), (0, 1, 3), (0, 3, 4), (1, 0, 2), (1, 2, 3), (1, 3, 4)]
+        for i, (b, t0, t1) in enumerate(pieces):
+            cols = slice(b * SH, (b + 1) * SH)
+            acc = bank(i, [P, t1 - t0, SH])
+            for t in range(t0, t1):
+                mm(acc[:, t - t0, :], w3_c, w3_s, t, z2_c[b][:], z2_s[b][:])
+            o = sb("o%d" % i, [P, t1 - t0, SH], F32)
+            nc.vector.tensor_tensor(o[:], acc[:], res_t[:, t0:t1, cols], ADD)
+            nc.sync.dma_start(out=out_rows[:, t0:t1, cols], in_=o[:])

@@ -44,7 +44,9 @@ def tile_picked_poolback_none_p_kernel(tc, x_words, x_scales, w1, w2, w3, res, o
             nc.sync.dma_start(out=raw[:], in_=w.rearrange("(p j) c -> p j c", j=PACK)[:, :, a * 256 : (a + 1) * 256])
             return raw
 
-        w1_raw = [load_half("w1", w1, a) for a in range(2)]
+        w1_raw = [sb("w1_raw%d" % a, [P, 2, H], F32) for a in range(2)]
+        for a in range(2):
+            nc.sync.dma_start(out=w1_raw[a][:], in_=w1.rearrange("(p j) c -> p j c", j=PACK)[:, 2 * a : 2 * a + 2, :])
         order_t = lists.tile([P, S // 16], U16, name="order_t")
         nc.sync.dma_start(order_t[:], order)
         w2_raw = [load_half("w2", w2, 0)]
@@ -80,17 +82,26 @@ def tile_picked_poolback_none_p_kernel(tc, x_words, x_scales, w1, w2, w3, res, o
                                 rhs=rc.bitcast(FP8X4), rhs_scale=rs, start=True, stop=True)
 
         w1_b = [sb("dealt", [P, 2, P, PACK], BF16), sb("w1_b1", [P, 2, P, PACK], BF16)]
-        deal(nc.scalar.copy, w1_b[0][:], w1_raw[0], 0, 0, 2)
-        deal(nc.scalar.copy, w1_b[1][:], w1_raw[0], 0, 2, 4)
-        deal(nc.vector.tensor_copy, w1_b[0][:], w1_raw[1], 1, 0, 2)
-        deal(nc.scalar.copy, w1_b[1][:], w1_raw[1], 1, 2, 4)
+
+        def deal_rows(copy, u, a):
+            copy(
+                out=w1_b[u][:].rearrange("p i m j -> p m j i")[:, :, 2 * a : 2 * a + 2, :],
+                in_=w1_raw[a][:].rearrange("p j (m t) -> p m j t", t=PACK)[:, :, :, 2 * u : 2 * u + 2],
+            )
+
+        deal_rows(nc.scalar.copy, 0, 0)
+        deal_rows(nc.scalar.copy, 1, 0)
+        deal_rows(nc.vector.tensor_copy, 0, 1)
+        deal_rows(nc.scalar.copy, 1, 1)
         w1_c = sb("w1_c", [P, H], U32)
         w1_s = sb("w1_s", [P, H], U8)
         for t0, t1 in [(0, 1), (1, 2), (2, 4)]:
             quantize(w1_c[:, t0 * P : t1 * P], w1_s[:, t0 * P : t1 * P],
                      w1_b[t0 // 2][:, t0 % 2 : t0 % 2 + t1 - t0].rearrange("p i m j -> p (i m j)"))
         SH = S // 2
-        y = [sb("y%d" % t, [P, S], F32) for t in range(PACK)]
+        y = [sb("y%d" % t, [P, 2 * S], F32) for t in range(PACK)]
+        for t in range(PACK):
+            nc.gpsimd.memset(y[t][:, S:], 0.0)
         for b in range(2):
             cols = slice(b * SH, (b + 1) * SH)
             acc = bank(4 * b, [P, SH])
@@ -99,7 +110,7 @@ def tile_picked_poolback_none_p_kernel(tc, x_words, x_scales, w1, w2, w3, res, o
         for t in range(1, PACK):
             acc = bank(t, [P, S])
             mm(acc[:], w1_c, w1_s, t, xg_w[:], xg_s[:])
-            nc.scalar.copy(out=y[t][:], in_=acc[:])
+            nc.scalar.copy(out=y[t][:, :S], in_=acc[:])
 
         w2_b = sb("dealt", [P, PACK, P, PACK], BF16)
         deal(nc.vector.tensor_copy, w2_b[:], w2_raw[0], 0, 0, 4)
@@ -117,35 +128,24 @@ def tile_picked_poolback_none_p_kernel(tc, x_words, x_scales, w1, w2, w3, res, o
         VH = V // 2
         quantize(w2_c[:], w2_s[:], w2_b[:].rearrange("p t m j -> p (t m j)"))
         h = sb("h", [P, PACK, V], F32)
-        g = sb("g", [P, PACK, 2 * VH], BF16)
-        z = [sb("z%d" % a, [P, VH, PACK], BF16) for a in range(2)]
-
-        def gather(a, t):
-            nc.vector.tensor_copy(g[:, t, :], y[t][:].indirect(order_t[:, 16 * a : 16 * a + 16]))
-
-        def pool_pairs(a):
-            pairs = g[:].rearrange("p t (c i e) -> p c t i e", i=4, e=2)
-            nc.vector.tensor_tensor(z[a][:].rearrange("p (c i) t -> p c t i", i=4), pairs[:, :, :, :, 0], pairs[:, :, :, :, 1], MAX)
-
-        def second(a):
-            z_c = sb("z_c%d" % a, [P, VH], U32)
-            z_s = sb("z_s%d" % a, [P, VH], U8)
-            quantize(z_c[:], z_s[:], z[a][:].rearrange("p v t -> p (v t)"))
-            for i, (t0, t1) in enumerate([(0, PACK)] if a == 0 else [(0, 1), (1, PACK)]):
-                acc = bank(5 + a + i, [P, t1 - t0, VH])
-                for t in range(t0, t1):
-                    mm(acc[:, t - t0, :], w2_c, w2_s, t, z_c[:], z_s[:])
-                nc.scalar.activation(h[:, t0:t1, a * VH : (a + 1) * VH], acc[:], RELU)
-
+        g = sb("g", [P, PACK, S], BF16)
         for t in range(PACK):
-            gather(0, t)
-        pool_pairs(0)
-        gather(1, 0)
-        second(0)
-        for t in range(1, PACK):
-            gather(1, t)
-        pool_pairs(1)
-        second(1)
+            nc.vector.tensor_copy(g[:, t, :], y[t][:].indirect(order_t[:]))
+        z = sb("dealt", [P, V, PACK], BF16)
+        z_c = sb("z_c", [P, V], U32)
+        z_s = sb("z_s", [P, V], U8)
+        pairs = g[:].rearrange("p t (c i e) -> p c t i e", i=4, e=2)
+        for a in range(2):
+            cs = slice(a * VH // 4, (a + 1) * VH // 4)
+            nc.vector.tensor_tensor(z[:].rearrange("p (c i) t -> p c t i", i=4)[:, cs], pairs[:, cs, :, :, 0], pairs[:, cs, :, :, 1], MAX)
+        for a in range(2):
+            vs = slice(a * VH, (a + 1) * VH)
+            quantize(z_c[:, vs], z_s[:, vs], z[:, vs, :].rearrange("p v t -> p (v t)"))
+        for t in range(PACK):
+            acc = bank(4 + t, [P, V])
+            for v0, v1 in ([(0, VH), (VH, V)] if t == 0 else [(0, V)]):
+                mm(acc[:, v0:v1], w2_c, w2_s, t, z_c[:, v0:v1], z_s[:, v0:v1])
+            nc.scalar.activation(h[:, t, :], acc[:], RELU)
 
         w3_c = sb("w3_c", [P, N], U32)
         w3_s = sb("w3_s", [P, N], U8)
@@ -159,11 +159,8 @@ def tile_picked_poolback_none_p_kernel(tc, x_words, x_scales, w1, w2, w3, res, o
         def weave(copy, b, t):
             copy(out=z2[b][:, :, t], in_=y[t][:, b * SH : (b + 1) * SH])
 
-        scatter(0, 0, VH)
-        scatter(0, VH, V)
         for t in range(PACK):
-            if t > 0:
-                scatter(t, 0, V)
+            scatter(t, 0, V)
             if t == 2:
                 nc.scalar.copy(out=z2[0][:, :, 2:4], in_=y[2][:, :SH].unsqueeze(2).to_broadcast([P, SH, 2]))
             elif t == 3:
@@ -173,16 +170,17 @@ def tile_picked_poolback_none_p_kernel(tc, x_words, x_scales, w1, w2, w3, res, o
             weave(nc.scalar.copy, 1, t)
 
         out_rows = out.rearrange("(t p) s -> p t s", p=P)
-        z2_c = [sb("z2_c%d" % b, [P, SH], U32) for b in range(2)]
-        z2_s = [sb("z2_s%d" % b, [P, SH], U8) for b in range(2)]
+        z2_c = sb("z2_c", [P, S], U32)
+        z2_s = sb("z2_s", [P, S], U8)
         for b in range(2):
-            quantize(z2_c[b][:], z2_s[b][:], z2[b][:].rearrange("p s t -> p (s t)"))
+            cols = slice(b * SH, (b + 1) * SH)
+            quantize(z2_c[:, cols], z2_s[:, cols], z2[b][:].rearrange("p s t -> p (s t)"))
         pieces = [(0, 0, 1), (0, 1, 3), (0, 3, 4), (1, 0, 2), (1, 2, 3), (1, 3, 4)]
         for i, (b, t0, t1) in enumerate(pieces):
             cols = slice(b * SH, (b + 1) * SH)
             acc = bank(i, [P, t1 - t0, SH])
             for t in range(t0, t1):
-                mm(acc[:, t - t0, :], w3_c, w3_s, t, z2_c[b][:], z2_s[b][:])
+                mm(acc[:, t - t0, :], w3_c, w3_s, t, z2_c[:, cols], z2_s[:, cols])
             o = sb("o%d" % i, [P, t1 - t0, SH], F32)
             nc.vector.tensor_tensor(o[:], acc[:], res_t[:, t0:t1, cols], ADD)
             nc.sync.dma_start(out=out_rows[:, t0:t1, cols], in_=o[:])

@@ -101,7 +101,7 @@ def tile_picked_poolback_none_p_kernel(tc, x_words, x_scales, w1, w2, w3, res, o
         SH = S // 2
         y = [sb("y%d" % t, [P, 2 * S], F32) for t in range(PACK)]
         for t in range(PACK):
-            nc.gpsimd.memset(y[t][:, S:], 0.0)
+            nc.vector.memset(y[t][:, S:], 0.0)
         for b in range(2):
             cols = slice(b * SH, (b + 1) * SH)
             acc = bank(4 * b, [P, SH])

@@ -18,6 +18,11 @@ RELU = mybir.ActivationFunctionType.Relu
 
 P = 128
 PACK = 4
+QUADRANT = 32
+LIST_ROWS = 16
+RUN = 4
+S_HALF = S // 2
+V_HALF = V // 2
 
 
 def tile_picked_poolback_none_p_kernel(tc, x_words, x_scales, w1, w2, w3, res, offs, order, at, out):
@@ -27,160 +32,163 @@ def tile_picked_poolback_none_p_kernel(tc, x_words, x_scales, w1, w2, w3, res, o
         keep = ctx.enter_context(tc.tile_pool(name="keep", bufs=1))
         psum = ctx.enter_context(tc.psum_pool(name="psum", bufs=1))
 
-        def sb(name, shape, dtype):
-            return keep.tile(shape, dtype, name=name, align_bytes=64)
-
-        xs = sb("xs", [P, T], U8)
-        nc.vector.memset(xs[:].bitcast(I32), 0)
-        xw = sb("xw", [P, T], I32)
-        nc.sync.dma_start(out=xw[:], in_=x_words[0].rearrange("p n t -> p (n t)").bitcast(I32))
-        for q in range(4):
-            nc.sync.dma_start(out=xs[32 * q : 32 * q + 4, :].bitcast(I32), in_=x_scales[0, 4 * q : 4 * q + 4, :].bitcast(I32))
-        offs_t = lists.tile([P, S // 16], U16, name="offs_t")
-        nc.sync.dma_start(offs_t[:], offs)
-
-        def load_half(name, w, a):
-            raw = sb("%s_raw%d" % (name, a), [P, PACK, H // 2], F32)
-            nc.sync.dma_start(out=raw[:], in_=w.rearrange("(p j) c -> p j c", j=PACK)[:, :, a * 256 : (a + 1) * 256])
-            return raw
-
-        w1_raw = [sb("w1_raw%d" % a, [P, 2, H], F32) for a in range(2)]
-        for a in range(2):
-            nc.sync.dma_start(out=w1_raw[a][:], in_=w1.rearrange("(p j) c -> p j c", j=PACK)[:, 2 * a : 2 * a + 2, :])
-        order_t = lists.tile([P, S // 16], U16, name="order_t")
-        nc.sync.dma_start(order_t[:], order)
-        w2_raw = [load_half("w2", w2, 0)]
-        at_t = lists.tile([P, V // 16], U16, name="at_t")
-        nc.sync.dma_start(at_t[:], at)
-        res_rows = res.rearrange("(t p) s -> p t s", p=P)
-        res_t = sb("res_t", [P, PACK, S], F32)
-        nc.sync.dma_start(out=res_t[:, 0, :], in_=res_rows[:, 0, :])
-        w2_raw.append(load_half("w2", w2, 1))
-        w3_raw = sb("w3_raw", [P, PACK, N], F32)
-        nc.sync.dma_start(out=w3_raw[:], in_=w3.rearrange("(p j) c -> p j c", j=PACK))
-        nc.sync.dma_start(out=res_t[:, 1:, :], in_=res_rows[:, 1:, :])
-
-        xg_s = sb("xg_s", [P, S], U8)
-        xg_w = sb("xg_w", [P, S], U32)
-        nc.vector.tensor_copy(xg_w[:], xw[:].bitcast(U32).indirect(offs_t[:]))
-        nc.vector.tensor_copy(xg_s[:], xs[:].indirect(offs_t[:]))
-
-        def deal(copy, dst, raw, a, t0, t1):
-            copy(
-                out=dst.rearrange("p i m j -> p m j i")[:, 64 * a : 64 * a + 64],
-                in_=raw[:].rearrange("p j (m t) -> p m j t", t=PACK)[:, :, :, t0:t1],
-            )
-
-        def quantize(codes, scales, src):
-            nc.vector.quantize_mx(out=codes.bitcast(FP8X4), scales=scales, in_=src)
+        def sbuf(name, shape, dtype, buffer=None):
+            return keep.tile(shape, dtype, name=name, tag=buffer or name, align_bytes=64)
 
         def bank(i, shape):
             return psum.tile(shape, F32, name="bank%d" % i)
 
-        def mm(acc, wc, ws, t, rc, rs):
-            nc.tensor.matmul_mx(out=acc, lhsT=wc[:, t * P : (t + 1) * P].bitcast(FP8X4), lhsT_scale=ws[:, t * P : (t + 1) * P],
-                                rhs=rc.bitcast(FP8X4), rhs_scale=rs, start=True, stop=True)
+        def quantize(codes, scales, values):
+            nc.vector.quantize_mx(out=codes.bitcast(FP8X4), scales=scales, in_=values)
 
-        w1_b = [sb("dealt", [P, 2, P, PACK], BF16), sb("w1_b1", [P, 2, P, PACK], BF16)]
+        def product(acc, w_codes, w_scales, tile, codes, scales):
+            cols = slice(tile * P, (tile + 1) * P)
+            nc.tensor.matmul_mx(out=acc, lhsT=w_codes[:, cols].bitcast(FP8X4), lhsT_scale=w_scales[:, cols],
+                                rhs=codes.bitcast(FP8X4), rhs_scale=scales, start=True, stop=True)
 
-        def deal_rows(copy, u, a):
+        def by_words(w):
+            return w.rearrange("(p j) c -> p j c", j=PACK)
+
+        scale_table = sbuf("scale_table", [P, T], U8)
+        nc.vector.memset(scale_table[:].bitcast(I32), 0)
+        word_table = sbuf("word_table", [P, T], I32)
+        nc.sync.dma_start(out=word_table[:], in_=x_words[0].rearrange("p n t -> p (n t)").bitcast(I32))
+        for q in range(P // QUADRANT):
+            nc.sync.dma_start(out=scale_table[QUADRANT * q : QUADRANT * q + PACK, :].bitcast(I32),
+                              in_=x_scales[0, PACK * q : PACK * (q + 1), :].bitcast(I32))
+        offs_list = lists.tile([P, S // LIST_ROWS], U16, name="offs_list")
+        nc.sync.dma_start(offs_list[:], offs)
+        w1_raw = [sbuf("w1_raw%d" % a, [P, 2, H], F32) for a in range(2)]
+        for a in range(2):
+            nc.sync.dma_start(out=w1_raw[a][:], in_=by_words(w1)[:, 2 * a : 2 * a + 2, :])
+        order_list = lists.tile([P, S // LIST_ROWS], U16, name="order_list")
+        nc.sync.dma_start(order_list[:], order)
+        w2_raw = [sbuf("w2_raw%d" % a, [P, PACK, H // 2], F32) for a in range(2)]
+        nc.sync.dma_start(out=w2_raw[0][:], in_=by_words(w2)[:, :, : H // 2])
+        at_list = lists.tile([P, V // LIST_ROWS], U16, name="at_list")
+        nc.sync.dma_start(at_list[:], at)
+        res_rows = res.rearrange("(t p) s -> p t s", p=P)
+        res_sb = sbuf("res_sb", [P, PACK, S], F32)
+        nc.sync.dma_start(out=res_sb[:, 0, :], in_=res_rows[:, 0, :])
+        nc.sync.dma_start(out=w2_raw[1][:], in_=by_words(w2)[:, :, H // 2 :])
+        w3_raw = sbuf("w3_raw", [P, PACK, N], F32)
+        nc.sync.dma_start(out=w3_raw[:], in_=by_words(w3))
+        nc.sync.dma_start(out=res_sb[:, 1:, :], in_=res_rows[:, 1:, :])
+
+        x_scale = sbuf("x_scale", [P, S], U8)
+        x_code = sbuf("x_code", [P, S], U32)
+        nc.vector.tensor_copy(x_code[:], word_table[:].bitcast(U32).indirect(offs_list[:]))
+        nc.vector.tensor_copy(x_scale[:], scale_table[:].indirect(offs_list[:]))
+
+        w1_dealt = [sbuf("w1_dealt0", [P, 2, P, PACK], BF16, "staging_a"), sbuf("w1_dealt1", [P, 2, P, PACK], BF16, "staging_b")]
+
+        def deal_w1(copy, u, a):
             copy(
-                out=w1_b[u][:].rearrange("p i m j -> p m j i")[:, :, 2 * a : 2 * a + 2, :],
+                out=w1_dealt[u][:].rearrange("p i m j -> p m j i")[:, :, 2 * a : 2 * a + 2, :],
                 in_=w1_raw[a][:].rearrange("p j (m t) -> p m j t", t=PACK)[:, :, :, 2 * u : 2 * u + 2],
             )
 
-        deal_rows(nc.scalar.copy, 0, 0)
-        deal_rows(nc.scalar.copy, 1, 0)
-        deal_rows(nc.vector.tensor_copy, 0, 1)
-        deal_rows(nc.scalar.copy, 1, 1)
-        w1_c = sb("w1_c", [P, H], U32)
-        w1_s = sb("w1_s", [P, H], U8)
+        deal_w1(nc.scalar.copy, 0, 0)
+        deal_w1(nc.scalar.copy, 1, 0)
+        deal_w1(nc.vector.tensor_copy, 0, 1)
+        deal_w1(nc.scalar.copy, 1, 1)
+        w1_code = sbuf("w1_code", [P, H], U32)
+        w1_scale = sbuf("w1_scale", [P, H], U8)
         for t0, t1 in [(0, 1), (1, 2), (2, 4)]:
-            quantize(w1_c[:, t0 * P : t1 * P], w1_s[:, t0 * P : t1 * P],
-                     w1_b[t0 // 2][:, t0 % 2 : t0 % 2 + t1 - t0].rearrange("p i m j -> p (i m j)"))
-        SH = S // 2
-        y = [sb("y%d" % t, [P, 2 * S], F32) for t in range(PACK)]
+            quantize(w1_code[:, t0 * P : t1 * P], w1_scale[:, t0 * P : t1 * P],
+                     w1_dealt[t0 // 2][:, t0 % 2 : t0 % 2 + t1 - t0].rearrange("p i m j -> p (i m j)"))
+
+        y = [sbuf("y%d" % t, [P, 2 * S], F32) for t in range(PACK)]
         for t in range(PACK):
             nc.vector.memset(y[t][:, S:], 0.0)
         for b in range(2):
-            cols = slice(b * SH, (b + 1) * SH)
-            acc = bank(4 * b, [P, SH])
-            mm(acc[:], w1_c, w1_s, 0, xg_w[:, cols], xg_s[:, cols])
+            cols = slice(b * S_HALF, (b + 1) * S_HALF)
+            acc = bank(PACK * b, [P, S_HALF])
+            product(acc[:], w1_code, w1_scale, 0, x_code[:, cols], x_scale[:, cols])
             nc.scalar.copy(out=y[0][:, cols], in_=acc[:])
         for t in range(1, PACK):
             acc = bank(t, [P, S])
-            mm(acc[:], w1_c, w1_s, t, xg_w[:], xg_s[:])
+            product(acc[:], w1_code, w1_scale, t, x_code[:], x_scale[:])
             nc.scalar.copy(out=y[t][:, :S], in_=acc[:])
 
-        w2_b = sb("dealt", [P, PACK, P, PACK], BF16)
-        deal(nc.vector.tensor_copy, w2_b[:], w2_raw[0], 0, 0, 4)
-        deal(nc.scalar.copy, w2_b[:], w2_raw[1], 1, 0, 4)
-        w2_c = sb("w2_c", [P, H], U32)
-        w2_s = sb("w2_s", [P, H], U8)
+        w2_first = sbuf("w2_first", [P, 1, P, PACK], BF16, "staging_a")
+        w2_rest = sbuf("w2_rest", [P, PACK - 1, P, PACK], BF16, "staging_b")
+        for a, copy in enumerate([nc.vector.tensor_copy, nc.scalar.copy]):
+            for dealt, t0, t1 in [(w2_first, 0, 1), (w2_rest, 1, PACK)]:
+                copy(
+                    out=dealt[:].rearrange("p i m j -> p m j i")[:, a * P // 2 : (a + 1) * P // 2],
+                    in_=w2_raw[a][:].rearrange("p j (m t) -> p m j t", t=PACK)[:, :, :, t0:t1],
+                )
+        w2_first_code = sbuf("w2_first_code", [P, P], U32)
+        w2_first_scale = sbuf("w2_first_scale", [P, P], U8)
 
-        w3_b = sb("w3_b", [P, N, PACK], BF16)
-        for a in range(4):
+        w3_woven = sbuf("w3_woven", [P, N, PACK], BF16)
+        for t in range(PACK):
+            cols = slice(t * P, (t + 1) * P)
             nc.scalar.copy(
-                out=w3_b[:, a * P : (a + 1) * P, :].rearrange("p (c i) j -> p c j i", i=4),
-                in_=w3_raw[:, :, a * P : (a + 1) * P].rearrange("p j (c i) -> p c j i", i=4),
+                out=w3_woven[:, cols, :].rearrange("p (c i) j -> p c j i", i=RUN),
+                in_=w3_raw[:, :, cols].rearrange("p j (c i) -> p c j i", i=RUN),
             )
 
-        VH = V // 2
-        quantize(w2_c[:], w2_s[:], w2_b[:].rearrange("p t m j -> p (t m j)"))
-        h = sb("h", [P, PACK, V], F32)
-        g = sb("g", [P, PACK, S], BF16)
+        quantize(w2_first_code[:], w2_first_scale[:], w2_first[:].rearrange("p t m j -> p (t m j)"))
+        h = sbuf("h", [P, PACK, V], F32)
+        lined_up = sbuf("lined_up", [P, PACK, S], BF16, "staging_c")
         for t in range(PACK):
-            nc.vector.tensor_copy(g[:, t, :], y[t][:].indirect(order_t[:]))
-        z = sb("dealt", [P, V, PACK], BF16)
-        z_c = sb("z_c", [P, V], U32)
-        z_s = sb("z_s", [P, V], U8)
-        pairs = g[:].rearrange("p t (c i e) -> p c t i e", i=4, e=2)
+            nc.vector.tensor_copy(lined_up[:, t, :], y[t][:].indirect(order_list[:]))
+        z = sbuf("z", [P, V, PACK], BF16, "staging_a")
+        z_code = sbuf("z_code", [P, V], U32)
+        z_scale = sbuf("z_scale", [P, V], U8)
+        pairs = lined_up[:].rearrange("p t (c i e) -> p c t i e", i=RUN, e=2)
         for a in range(2):
-            cs = slice(a * VH // 4, (a + 1) * VH // 4)
-            nc.vector.tensor_tensor(z[:].rearrange("p (c i) t -> p c t i", i=4)[:, cs], pairs[:, cs, :, :, 0], pairs[:, cs, :, :, 1], MAX)
+            runs = slice(a * V_HALF // RUN, (a + 1) * V_HALF // RUN)
+            nc.vector.tensor_tensor(z[:].rearrange("p (c i) t -> p c t i", i=RUN)[:, runs],
+                                    pairs[:, runs, :, :, 0], pairs[:, runs, :, :, 1], MAX)
         for a in range(2):
-            vs = slice(a * VH, (a + 1) * VH)
-            quantize(z_c[:, vs], z_s[:, vs], z[:, vs, :].rearrange("p v t -> p (v t)"))
-        for t in range(PACK):
-            acc = bank(4 + t, [P, V])
-            for v0, v1 in ([(0, VH), (VH, V)] if t == 0 else [(0, V)]):
-                mm(acc[:, v0:v1], w2_c, w2_s, t, z_c[:, v0:v1], z_s[:, v0:v1])
+            pooled = slice(a * V_HALF, (a + 1) * V_HALF)
+            quantize(z_code[:, pooled], z_scale[:, pooled], z[:, pooled, :].rearrange("p v t -> p (v t)"))
+
+        acc = bank(PACK, [P, V])
+        for a in range(2):
+            pooled = slice(a * V_HALF, (a + 1) * V_HALF)
+            product(acc[:, pooled], w2_first_code, w2_first_scale, 0, z_code[:, pooled], z_scale[:, pooled])
+        nc.scalar.activation(h[:, 0, :], acc[:], RELU)
+        w2_rest_code = sbuf("w2_rest_code", [P, (PACK - 1) * P], U32, "staging_c")
+        w2_rest_scale = sbuf("w2_rest_scale", [P, (PACK - 1) * P], U8)
+        for i0, i1 in [(0, 1), (1, 3)]:
+            quantize(w2_rest_code[:, i0 * P : i1 * P], w2_rest_scale[:, i0 * P : i1 * P],
+                     w2_rest[:, i0:i1].rearrange("p t m j -> p (t m j)"))
+        for t in range(1, PACK):
+            acc = bank(PACK + t, [P, V])
+            product(acc[:], w2_rest_code, w2_rest_scale, t - 1, z_code[:], z_scale[:])
             nc.scalar.activation(h[:, t, :], acc[:], RELU)
+        w3_code = sbuf("w3_code", [P, N], U32)
+        w3_scale = sbuf("w3_scale", [P, N], U8)
+        quantize(w3_code[:], w3_scale[:], w3_woven[:].rearrange("p n j -> p (n j)"))
 
-        w3_c = sb("w3_c", [P, N], U32)
-        w3_s = sb("w3_s", [P, N], U8)
-        quantize(w3_c[:], w3_s[:], w3_b[:].rearrange("p n j -> p (n j)"))
-
-        z2 = [sb("z2_%d" % b, [P, SH, PACK], BF16) for b in range(2)]
-
-        def scatter(t, v0, v1):
-            nc.vector.tensor_copy(y[t][:].indirect(at_t[:, v0 // 16 : v1 // 16]), h[:, t, v0:v1])
-
-        def weave(copy, b, t):
-            copy(out=z2[b][:, :, t], in_=y[t][:, b * SH : (b + 1) * SH])
-
+        z2 = [sbuf("z2_%d" % b, [P, S_HALF, PACK], BF16) for b in range(2)]
+        last = PACK - 1
         for t in range(PACK):
-            scatter(t, 0, V)
-            if t == 2:
-                nc.scalar.copy(out=z2[0][:, :, 2:4], in_=y[2][:, :SH].unsqueeze(2).to_broadcast([P, SH, 2]))
-            elif t == 3:
-                weave(nc.vector.tensor_copy, 0, t)
+            nc.vector.tensor_copy(y[t][:].indirect(at_list[:]), h[:, t, :])
+            if t == last:
+                nc.vector.tensor_copy(out=z2[0][:, :, t], in_=y[t][:, :S_HALF])
+            elif t == last - 1:
+                nc.scalar.copy(out=z2[0][:, :, t:], in_=y[t][:, :S_HALF].unsqueeze(2).to_broadcast([P, S_HALF, 2]))
             else:
-                weave(nc.scalar.copy, 0, t)
-            weave(nc.scalar.copy, 1, t)
+                nc.scalar.copy(out=z2[0][:, :, t], in_=y[t][:, :S_HALF])
+            nc.scalar.copy(out=z2[1][:, :, t], in_=y[t][:, S_HALF:S])
 
         out_rows = out.rearrange("(t p) s -> p t s", p=P)
-        z2_c = sb("z2_c", [P, S], U32)
-        z2_s = sb("z2_s", [P, S], U8)
+        z2_code = sbuf("z2_code", [P, S], U32)
+        z2_scale = sbuf("z2_scale", [P, S], U8)
         for b in range(2):
-            cols = slice(b * SH, (b + 1) * SH)
-            quantize(z2_c[:, cols], z2_s[:, cols], z2[b][:].rearrange("p s t -> p (s t)"))
+            cols = slice(b * S_HALF, (b + 1) * S_HALF)
+            quantize(z2_code[:, cols], z2_scale[:, cols], z2[b][:].rearrange("p s t -> p (s t)"))
         pieces = [(0, 0, 1), (0, 1, 3), (0, 3, 4), (1, 0, 2), (1, 2, 3), (1, 3, 4)]
         for i, (b, t0, t1) in enumerate(pieces):
-            cols = slice(b * SH, (b + 1) * SH)
-            acc = bank(i, [P, t1 - t0, SH])
+            cols = slice(b * S_HALF, (b + 1) * S_HALF)
+            acc = bank(i, [P, t1 - t0, S_HALF])
             for t in range(t0, t1):
-                mm(acc[:, t - t0, :], w3_c, w3_s, t, z2_c[:, cols], z2_s[:, cols])
-            o = sb("o%d" % i, [P, t1 - t0, SH], F32)
-            nc.vector.tensor_tensor(o[:], acc[:], res_t[:, t0:t1, cols], ADD)
-            nc.sync.dma_start(out=out_rows[:, t0:t1, cols], in_=o[:])
+                product(acc[:, t - t0, :], w3_code, w3_scale, t, z2_code[:, cols], z2_scale[:, cols])
+            total = sbuf("total%d" % i, [P, t1 - t0, S_HALF], F32)
+            nc.vector.tensor_tensor(total[:], acc[:], res_sb[:, t0:t1, cols], ADD)
+            nc.sync.dma_start(out=out_rows[:, t0:t1, cols], in_=total[:])

from contextlib import ExitStack

import concourse.mybir as mybir

K, T, S, V, N, H = 512, 2048, 512, 256, 512, 512
FLOPS = 2 * K * H * S + 2 * H * H * V + 2 * H * N * S

F32 = mybir.dt.float32
BF16 = mybir.dt.bfloat16
I32 = mybir.dt.int32
U32 = mybir.dt.uint32
U16 = mybir.dt.uint16
U8 = mybir.dt.uint8
FP8X4 = mybir.dt.float8_e4m3fn_x4
MAX = mybir.AluOpType.max
ADD = mybir.AluOpType.add
RELU = mybir.ActivationFunctionType.Relu

P = 128
PACK = 4
QUADRANT = 32
LIST_ROWS = 16
RUN = 4
S_HALF = S // 2
V_HALF = V // 2


def tile_picked_poolback_none_p_kernel(tc, x_words, x_scales, w1, w2, w3, res, offs, order, at, out):
    nc = tc.nc
    with ExitStack() as ctx:
        lists = ctx.enter_context(tc.tile_pool(name="lists", bufs=1))
        keep = ctx.enter_context(tc.tile_pool(name="keep", bufs=1))
        psum = ctx.enter_context(tc.psum_pool(name="psum", bufs=1))

        def sbuf(name, shape, dtype, buffer=None):
            return keep.tile(shape, dtype, name=name, tag=buffer or name, align_bytes=64)

        def bank(i, shape):
            return psum.tile(shape, F32, name="bank%d" % i)

        def quantize(codes, scales, values):
            nc.vector.quantize_mx(out=codes.bitcast(FP8X4), scales=scales, in_=values)

        def product(acc, w_codes, w_scales, tile, codes, scales):
            cols = slice(tile * P, (tile + 1) * P)
            nc.tensor.matmul_mx(out=acc, lhsT=w_codes[:, cols].bitcast(FP8X4), lhsT_scale=w_scales[:, cols],
                                rhs=codes.bitcast(FP8X4), rhs_scale=scales, start=True, stop=True)

        def by_words(w):
            return w.rearrange("(p j) c -> p j c", j=PACK)

        scale_table = sbuf("scale_table", [P, T], U8)
        nc.vector.memset(scale_table[:].bitcast(I32), 0)
        word_table = sbuf("word_table", [P, T], I32)
        nc.sync.dma_start(out=word_table[:], in_=x_words[0].rearrange("p n t -> p (n t)").bitcast(I32))
        for q in range(P // QUADRANT):
            nc.sync.dma_start(out=scale_table[QUADRANT * q : QUADRANT * q + PACK, :].bitcast(I32),
                              in_=x_scales[0, PACK * q : PACK * (q + 1), :].bitcast(I32))
        offs_list = lists.tile([P, S // LIST_ROWS], U16, name="offs_list")
        nc.sync.dma_start(offs_list[:], offs)
        w1_raw = [sbuf("w1_raw%d" % a, [P, 2, H], F32) for a in range(2)]
        for a in range(2):
            nc.sync.dma_start(out=w1_raw[a][:], in_=by_words(w1)[:, 2 * a : 2 * a + 2, :])
        order_list = lists.tile([P, S // LIST_ROWS], U16, name="order_list")
        nc.sync.dma_start(order_list[:], order)
        w2_raw = [sbuf("w2_raw%d" % a, [P, PACK, H // 2], F32) for a in range(2)]
        nc.sync.dma_start(out=w2_raw[0][:], in_=by_words(w2)[:, :, : H // 2])
        at_list = lists.tile([P, V // LIST_ROWS], U16, name="at_list")
        nc.sync.dma_start(at_list[:], at)
        res_rows = res.rearrange("(t p) s -> p t s", p=P)
        res_sb = sbuf("res_sb", [P, PACK, S], F32)
        nc.sync.dma_start(out=res_sb[:, 0, :], in_=res_rows[:, 0, :])
        nc.sync.dma_start(out=w2_raw[1][:], in_=by_words(w2)[:, :, H // 2 :])
        w3_raw = sbuf("w3_raw", [P, PACK, N], F32)
        nc.sync.dma_start(out=w3_raw[:], in_=by_words(w3))
        nc.sync.dma_start(out=res_sb[:, 1:, :], in_=res_rows[:, 1:, :])

        x_scale = sbuf("x_scale", [P, S], U8)
        x_code = sbuf("x_code", [P, S], U32)
        nc.vector.tensor_copy(x_code[:], word_table[:].bitcast(U32).indirect(offs_list[:]))
        nc.vector.tensor_copy(x_scale[:], scale_table[:].indirect(offs_list[:]))

        w1_dealt = [sbuf("w1_dealt0", [P, 2, P, PACK], BF16, "staging_a"), sbuf("w1_dealt1", [P, 2, P, PACK], BF16, "staging_b")]

        def deal_w1(copy, u, a):
            copy(
                out=w1_dealt[u][:].rearrange("p i m j -> p m j i")[:, :, 2 * a : 2 * a + 2, :],
                in_=w1_raw[a][:].rearrange("p j (m t) -> p m j t", t=PACK)[:, :, :, 2 * u : 2 * u + 2],
            )

        deal_w1(nc.scalar.copy, 0, 0)
        deal_w1(nc.scalar.copy, 1, 0)
        deal_w1(nc.vector.tensor_copy, 0, 1)
        deal_w1(nc.scalar.copy, 1, 1)
        w1_code = sbuf("w1_code", [P, H], U32)
        w1_scale = sbuf("w1_scale", [P, H], U8)
        for t0, t1 in [(0, 1), (1, 2), (2, 4)]:
            quantize(w1_code[:, t0 * P : t1 * P], w1_scale[:, t0 * P : t1 * P],
                     w1_dealt[t0 // 2][:, t0 % 2 : t0 % 2 + t1 - t0].rearrange("p i m j -> p (i m j)"))

        y = [sbuf("y%d" % t, [P, 2 * S], F32) for t in range(PACK)]
        for t in range(PACK):
            nc.vector.memset(y[t][:, S:], 0.0)
        for b in range(2):
            cols = slice(b * S_HALF, (b + 1) * S_HALF)
            acc = bank(PACK * b, [P, S_HALF])
            product(acc[:], w1_code, w1_scale, 0, x_code[:, cols], x_scale[:, cols])
            nc.scalar.copy(out=y[0][:, cols], in_=acc[:])
        for t in range(1, PACK):
            acc = bank(t, [P, S])
            product(acc[:], w1_code, w1_scale, t, x_code[:], x_scale[:])
            nc.scalar.copy(out=y[t][:, :S], in_=acc[:])

        w2_first = sbuf("w2_first", [P, 1, P, PACK], BF16, "staging_a")
        w2_rest = sbuf("w2_rest", [P, PACK - 1, P, PACK], BF16, "staging_b")
        for a, copy in enumerate([nc.vector.tensor_copy, nc.scalar.copy]):
            for dealt, t0, t1 in [(w2_first, 0, 1), (w2_rest, 1, PACK)]:
                copy(
                    out=dealt[:].rearrange("p i m j -> p m j i")[:, a * P // 2 : (a + 1) * P // 2],
                    in_=w2_raw[a][:].rearrange("p j (m t) -> p m j t", t=PACK)[:, :, :, t0:t1],
                )
        w2_first_code = sbuf("w2_first_code", [P, P], U32)
        w2_first_scale = sbuf("w2_first_scale", [P, P], U8)

        w3_woven = sbuf("w3_woven", [P, N, PACK], BF16)
        for t in range(PACK):
            cols = slice(t * P, (t + 1) * P)
            nc.scalar.copy(
                out=w3_woven[:, cols, :].rearrange("p (c i) j -> p c j i", i=RUN),
                in_=w3_raw[:, :, cols].rearrange("p j (c i) -> p c j i", i=RUN),
            )

        quantize(w2_first_code[:], w2_first_scale[:], w2_first[:].rearrange("p t m j -> p (t m j)"))
        h = sbuf("h", [P, PACK, V], F32)
        lined_up = sbuf("lined_up", [P, PACK, S], BF16, "staging_c")
        for t in range(PACK):
            nc.vector.tensor_copy(lined_up[:, t, :], y[t][:].indirect(order_list[:]))
        z = sbuf("z", [P, V, PACK], BF16, "staging_a")
        z_code = sbuf("z_code", [P, V], U32)
        z_scale = sbuf("z_scale", [P, V], U8)
        pairs = lined_up[:].rearrange("p t (c i e) -> p c t i e", i=RUN, e=2)
        for a in range(2):
            runs = slice(a * V_HALF // RUN, (a + 1) * V_HALF // RUN)
            nc.vector.tensor_tensor(z[:].rearrange("p (c i) t -> p c t i", i=RUN)[:, runs],
                                    pairs[:, runs, :, :, 0], pairs[:, runs, :, :, 1], MAX)
        for a in range(2):
            pooled = slice(a * V_HALF, (a + 1) * V_HALF)
            quantize(z_code[:, pooled], z_scale[:, pooled], z[:, pooled, :].rearrange("p v t -> p (v t)"))

        acc = bank(PACK, [P, V])
        for a in range(2):
            pooled = slice(a * V_HALF, (a + 1) * V_HALF)
            product(acc[:, pooled], w2_first_code, w2_first_scale, 0, z_code[:, pooled], z_scale[:, pooled])
        nc.scalar.activation(h[:, 0, :], acc[:], RELU)
        w2_rest_code = sbuf("w2_rest_code", [P, (PACK - 1) * P], U32, "staging_c")
        w2_rest_scale = sbuf("w2_rest_scale", [P, (PACK - 1) * P], U8)
        for i0, i1 in [(0, 1), (1, 3)]:
            quantize(w2_rest_code[:, i0 * P : i1 * P], w2_rest_scale[:, i0 * P : i1 * P],
                     w2_rest[:, i0:i1].rearrange("p t m j -> p (t m j)"))
        for t in range(1, PACK):
            acc = bank(PACK + t, [P, V])
            product(acc[:], w2_rest_code, w2_rest_scale, t - 1, z_code[:], z_scale[:])
            nc.scalar.activation(h[:, t, :], acc[:], RELU)
        w3_code = sbuf("w3_code", [P, N], U32)
        w3_scale = sbuf("w3_scale", [P, N], U8)
        quantize(w3_code[:], w3_scale[:], w3_woven[:].rearrange("p n j -> p (n j)"))

        z2 = [sbuf("z2_%d" % b, [P, S_HALF, PACK], BF16) for b in range(2)]
        last = PACK - 1
        for t in range(PACK):
            nc.vector.tensor_copy(y[t][:].indirect(at_list[:]), h[:, t, :])
            if t == last:
                nc.vector.tensor_copy(out=z2[0][:, :, t], in_=y[t][:, :S_HALF])
            elif t == last - 1:
                nc.scalar.copy(out=z2[0][:, :, t:], in_=y[t][:, :S_HALF].unsqueeze(2).to_broadcast([P, S_HALF, 2]))
            else:
                nc.scalar.copy(out=z2[0][:, :, t], in_=y[t][:, :S_HALF])
            nc.scalar.copy(out=z2[1][:, :, t], in_=y[t][:, S_HALF:S])

        out_rows = out.rearrange("(t p) s -> p t s", p=P)
        z2_code = sbuf("z2_code", [P, S], U32)
        z2_scale = sbuf("z2_scale", [P, S], U8)
        for b in range(2):
            cols = slice(b * S_HALF, (b + 1) * S_HALF)
            quantize(z2_code[:, cols], z2_scale[:, cols], z2[b][:].rearrange("p s t -> p (s t)"))
        pieces = [(0, 0, 1), (0, 1, 3), (0, 3, 4), (1, 0, 2), (1, 2, 3), (1, 3, 4)]
        for i, (b, t0, t1) in enumerate(pieces):
            cols = slice(b * S_HALF, (b + 1) * S_HALF)
            acc = bank(i, [P, t1 - t0, S_HALF])
            for t in range(t0, t1):
                product(acc[:, t - t0, :], w3_code, w3_scale, t, z2_code[:, cols], z2_scale[:, cols])
            total = sbuf("total%d" % i, [P, t1 - t0, S_HALF], F32)
            nc.vector.tensor_tensor(total[:], acc[:], res_sb[:, t0:t1, cols], ADD)
            nc.sync.dma_start(out=out_rows[:, t0:t1, cols], in_=total[:])
